import numpy as np
import ml_dtypes


def mxq(x, axis, fmt="e4m3"):
    dtype, down = {"e4m3": (ml_dtypes.float8_e4m3fn, 7), "e5m2": (ml_dtypes.float8_e5m2, 14)}[fmt]
    v = np.moveaxis(np.asarray(x, np.float32).astype(ml_dtypes.bfloat16).astype(np.float64), axis, -1)
    blocks = v.reshape(v.shape[:-1] + (-1, 32))
    amax = np.abs(blocks).max(-1, keepdims=True)
    byte = np.maximum(np.where(amax > 0, np.frexp(amax)[1] - 1 + 127, 0) - down, 1)
    scale = np.exp2(byte - 127.0)
    codes = (blocks / scale).astype(np.float32).astype(dtype).astype(np.float64)
    return np.moveaxis((codes * scale).reshape(v.shape), -1, axis)


WIDE = False


def mx_kscale(k):
    if not WIDE:
        return np.ones(k)
    levels = np.array([30, -30])
    if k % 512:
        return np.exp2(np.random.permutation(np.resize(levels, k // 32))).repeat(32)
    a = np.empty((k // 512, 16))
    for p in range(k // 512):
        a[p, :8] = np.random.permutation(np.resize(levels, 8))
        for g in range(8):
            far = levels[np.abs(levels - a[p, g]) >= 10]
            a[p, g + 8] = far[np.random.randint(len(far))]
    return np.exp2(a.ravel()).repeat(32)


def f64(x):
    return np.asarray(x).astype(np.float64)


def striped(idx):
    return np.tile(np.asarray(idx).reshape(-1, 16).T, (8, 1)).astype(np.uint16)


def unstriped(offs):
    return offs[:16].T.reshape(-1).astype(np.int64)


E2M1 = np.array([0.0, 0.5, 1.0, 1.5, 2.0, 3.0, 4.0, 6.0, -0.0, -0.5, -1.0, -1.5, -2.0, -3.0, -4.0, -6.0])


def pack_weight(w, fmt):
    k, n = w.shape
    w = f64(np.asarray(w, np.float32).astype(ml_dtypes.bfloat16)).reshape(k // 32, 32, n)
    amax = np.abs(w).max(1)
    if fmt == "e4m3":
        byte = np.frexp(amax)[1] - 1 + 127 - 7
    else:
        mant, ex = np.frexp(amax / 6.0)
        byte = np.where(mant > 0.5, ex, ex - 1) + 127
    byte = np.clip(np.where(amax > 0, byte, 1), 1, 254)
    scaled = (w * np.exp2(127.0 - byte)[:, None, :]).reshape(k, n).astype(np.float32)
    by_word = np.ascontiguousarray(scaled.reshape(k // 512, 128, 4, n).transpose(0, 1, 3, 2))
    if fmt == "e4m3":
        words = by_word.astype(ml_dtypes.float8_e4m3fn).view(np.uint8)
    else:
        c = by_word.astype(ml_dtypes.float4_e2m1fn).view(np.uint8) & 0xF
        words = (c[..., 0::2] | (c[..., 1::2] << 4)).reshape(k // 512, 128, 2 * n)
    return np.ascontiguousarray(words), np.ascontiguousarray(byte.astype(np.uint8).reshape(k // 512, 16, n))


def unpack_weight(words, scales, fmt):
    g, _, n = scales.shape
    words = np.ascontiguousarray(words).reshape(g, 128, n, -1)
    if fmt == "e4m3":
        vals = words.view(ml_dtypes.float8_e4m3fn).astype(np.float64)
    else:
        nib = np.empty((g, 128, n, 4), np.uint8)
        nib[..., 0::2] = words & 0xF
        nib[..., 1::2] = words >> 4
        vals = E2M1[nib]
    vals = vals * np.repeat(np.exp2(scales.astype(np.float64) - 127.0), 8, axis=1)[..., None]
    return vals.transpose(0, 1, 3, 2).reshape(g * 512, n)


K, T, J, S, R, N = 1024, 1024, 256, 512, 512, 256


def setup_inputs():
    n = np.random.standard_normal
    idx = np.random.permutation(T)[:J]
    idx2 = np.random.permutation(S)[:J]
    fk = mx_kscale(K)
    fr = mx_kscale(R)
    wp = pack_weight(n((K, R)) * 1 / np.sqrt(K) * fk[:, None] * fr, "e2m1")
    wbp = pack_weight(n((R, N)) * 1 / np.sqrt(R) / fr[:, None], "e4m3")
    return {
        "xa": (n((K, T))).astype(np.float32),
        "xb": (n((K, S))).astype(np.float32),
        "fk": (np.random.uniform(0.5, 2.0, (K, 1)) / fk[:, None]).astype(np.float32),
        "w_words": wp[0],
        "w_scales": wp[1],
        "us": (np.random.uniform(0.5, 2.0, (R, 1)) * fr[:, None]).astype(np.float32),
        "wb_words": wbp[0],
        "wb_scales": wbp[1],
        "bi": (np.random.uniform(-0.5, 0.5, (1, N))).astype(np.float32),
        "offs": striped(idx),
        "offs2": striped(idx2),
    }


def reference(xa, xb, fk, w_words, w_scales, us, wb_words, wb_scales, bi, offs, offs2):
    idx = unstriped(offs)
    idx2 = unstriped(offs2)
    wu = unpack_weight(w_words, w_scales, "e2m1")
    wbu = unpack_weight(wb_words, wb_scales, "e4m3")
    u = f64(xa)[:, idx] * f64(xb)[:, idx2] * f64(fk)
    uq = mxq(u, 0, "e4m3")
    a = wu.T @ uq
    pk1 = np.max(np.abs(a), axis=1, keepdims=True)
    hid = a / pk1 * f64(us)
    hidq = mxq(hid, 0, "e5m2")
    p = hidq.T @ wbu
    ea = np.exp(0.7 * p + f64(bi))
    y = 256.0 * ea / np.sum(ea, axis=1, keepdims=True)
    return y

@@ -1,0 +1,259 @@
+from contextlib import ExitStack
+
+import concourse.mybir as mybir
+from concourse.masks import make_identity
+
+K, T, J, S, R, N = 1024, 1024, 256, 512, 512, 256
+FLOPS = 2 * K * R * J + 2 * R * J * N
+
+F32 = mybir.dt.float32
+BF16 = mybir.dt.bfloat16
+I32 = mybir.dt.int32
+U32 = mybir.dt.uint32
+U16 = mybir.dt.uint16
+U8 = mybir.dt.uint8
+E4M3 = mybir.dt.float8_e4m3fn_x4
+E5M2 = mybir.dt.float8_e5m2_x4
+E2M1 = mybir.dt.float4_e2m1fn_x4
+ALU = mybir.AluOpType
+ACT = mybir.ActivationFunctionType
+AX = mybir.AxisListType
+
+P = 128
+PACK = 4
+PASSES = K // (P * PACK)
+HALVES = J // P
+LIST_COLS = J // 16
+
+
+def tile_list_entryproducts_peakscaled_rowshares_kernel(
+    tc, xa, xb, fk, w_words, w_scales, us, wb_words, wb_scales, bi, offs, offs2, out
+):
+    nc = tc.nc
+    with ExitStack() as ctx:
+        sb = ctx.enter_context(tc.tile_pool(name="sb", bufs=1))
+        ps = ctx.enter_context(tc.psum_pool(name="ps", bufs=1))
+
+        list_a = sb.tile([P, LIST_COLS], U16, name="list_a")
+        list_b = sb.tile([P, LIST_COLS], U16, name="list_b")
+        xa_t = [[sb.tile([P, T], F32, name="xa_%d_%d" % (z, t)) for t in range(PACK)] for z in range(PASSES)]
+        xb_t = [[sb.tile([P, 2, S], F32, name="xb_%d_%d" % (z, i)) for i in range(2)] for z in range(PASSES)]
+        fk_t = sb.tile([P, PASSES, PACK], F32, name="fk_t")
+        us_t = sb.tile([P, PACK], F32, name="us_t")
+        bi_col = sb.tile([P, 2], F32, name="bi_col")
+        w_raw = sb.tile([P, PASSES, R], U16, name="w_raw", align_bytes=64)
+        ws_raw = sb.tile([P, PASSES, R], U8, name="ws_raw", align_bytes=64)
+        wb_codes = sb.tile([P, N], U32, name="wb_codes", align_bytes=64)
+        wb_plane = sb.tile([P, N], U8, name="wb_plane", align_bytes=64)
+
+        nc.vector.memset(ws_raw[:].bitcast(I32), 0)
+        nc.vector.memset(wb_plane[:].bitcast(I32), 0)
+
+        xa_v = xa.rearrange("(z p t) c -> z t p c", p=P, t=PACK)
+        xb_v = xb.rearrange("(z p i e) c -> z i p e c", p=P, i=2, e=2)
+
+        def load_xa(z, t):
+            nc.sync.dma_start(out=xa_t[z][t][:], in_=xa_v[z, t])
+
+        def load_xb(z, i):
+            nc.sync.dma_start(out=xb_t[z][i][:], in_=xb_v[z, i])
+
+        def load_ws(q):
+            nc.sync.dma_start(
+                out=ws_raw[32 * q : 32 * q + 4].bitcast(I32),
+                in_=w_scales[:, 4 * q : 4 * q + 4, :].rearrange("z r c -> r z c").bitcast(I32),
+            )
+
+        def load_wbs(q):
+            nc.sync.dma_start(
+                out=wb_plane[32 * q : 32 * q + 4].bitcast(I32),
+                in_=wb_scales[0, 4 * q : 4 * q + 4, :].bitcast(I32),
+            )
+
+        load_xb(0, 0)
+        nc.sync.dma_start(list_b[:], offs2)
+        load_xb(0, 1)
+        nc.sync.dma_start(out=fk_t[:], in_=fk.rearrange("(z p t) o -> p z (t o)", p=P, t=PACK))
+        load_xa(0, 0)
+        nc.sync.dma_start(list_a[:], offs)
+        load_xa(0, 1)
+        nc.sync.dma_start(out=w_raw[:].bitcast(I32), in_=w_words.rearrange("z p c -> p z c").bitcast(I32))
+        load_xa(0, 2)
+        load_ws(0)
+        load_ws(1)
+        load_xa(0, 3)
+        load_ws(2)
+        load_ws(3)
+        load_xb(1, 0)
+        nc.sync.dma_start(out=bi_col[:], in_=bi.rearrange("o (p e) -> p (o e)", e=2))
+        nc.sync.dma_start(out=us_t[:], in_=us.rearrange("(p t) o -> p (t o)", t=PACK))
+        load_xb(1, 1)
+        nc.sync.dma_start(
+            out=wb_codes[:].bitcast(I32), in_=wb_words[0].rearrange("p n t -> p (n t)").bitcast(I32)
+        )
+        load_xa(1, 0)
+        load_wbs(0)
+        load_wbs(1)
+        load_xa(1, 1)
+        load_wbs(2)
+        load_wbs(3)
+        load_xa(1, 2)
+        load_xa(1, 3)
+
+        ident = sb.tile([P, P], F32, name="ident")
+        make_identity(nc, ident[:])
+
+        picked_b = [sb.tile([P, PACK, J], F32, name="picked_b%d" % z) for z in range(PASSES)]
+        scaled_b = [sb.tile([P, PACK, J], F32, name="scaled_b%d" % z) for z in range(PASSES)]
+        prod = [sb.tile([P, PACK, J], F32, name="prod%d" % z) for z in range(PASSES)]
+        u_bf = [
+            [sb.tile([P, P, PACK], BF16, name="u_bf%d_%d" % (z, h), align_bytes=64) for h in range(HALVES)]
+            for z in range(PASSES)
+        ]
+        u_codes = [
+            [sb.tile([P, P], U32, name="u_codes%d_%d" % (z, h), align_bytes=64) for h in range(HALVES)]
+            for z in range(PASSES)
+        ]
+        u_plane = [
+            [sb.tile([P, P], U8, name="u_plane%d_%d" % (z, h), align_bytes=64) for h in range(HALVES)]
+            for z in range(PASSES)
+        ]
+        w_codes = sb.tile([P, PASSES, R], U16, name="w_codes", align_bytes=64)
+        w_plane = sb.tile([P, PASSES, R], U8, name="w_plane", align_bytes=64)
+        a_ps = [ps.tile([P, PACK, P], F32, name="a_ps%d" % h) for h in range(HALVES)]
+        p_ps = [ps.tile([P, N], F32, name="p_ps%d" % h) for h in range(HALVES)]
+        bi_ps = ps.tile([P, 2, P], F32, name="bi_ps")
+        bi_row = sb.tile([P, N], F32, name="bi_row")
+
+        def cols(h):
+            return slice(h * P, (h + 1) * P)
+
+        def pick_b(z, t):
+            nc.scalar.activation(picked_b[z][:, t, :], xb_t[z][t // 2][:, t % 2, :].indirect(list_b[:]), ACT.Copy)
+            nc.scalar.activation(
+                scaled_b[z][:, t, :], picked_b[z][:, t, :], ACT.Copy, scale=fk_t[:, z, t : t + 1]
+            )
+
+        def product(z, t):
+            nc.vector.tensor_tensor(prod[z][:, t, :], xa_t[z][t][:].indirect(list_a[:]), scaled_b[z][:, t, :], ALU.mult)
+
+        def product_half(z, t, h):
+            half = LIST_COLS // HALVES
+            nc.vector.tensor_tensor(
+                prod[z][:, t, cols(h)],
+                xa_t[z][t][:].indirect(list_a[:, h * half : (h + 1) * half]),
+                scaled_b[z][:, t, cols(h)],
+                ALU.mult,
+            )
+
+        def round_u(copy, z, h, t0, t1):
+            copy(u_bf[z][h][:, :, t0:t1], prod[z][:, t0:t1, cols(h)].rearrange("p t j -> p j t"))
+
+        def quantize_u(z, h):
+            nc.vector.quantize_mx(
+                out=u_codes[z][h][:].bitcast(E4M3),
+                scales=u_plane[z][h][:],
+                in_=u_bf[z][h][:].rearrange("p j t -> p (j t)"),
+            )
+
+        def first_matmuls(z, h):
+            for t in range(PACK):
+                nc.tensor.matmul_mx(
+                    out=a_ps[h][:, t, :],
+                    lhsT=w_codes[:, z, cols(t)].bitcast(E2M1),
+                    lhsT_scale=w_plane[:, z, cols(t)],
+                    rhs=u_codes[z][h][:].bitcast(E4M3),
+                    rhs_scale=u_plane[z][h][:],
+                    start=(z == 0 and t == 0),
+                    stop=(z == PASSES - 1 and t == PACK - 1),
+                )
+
+        for t in range(PACK):
+            pick_b(0, t)
+            product(0, t)
+        nc.vector.tensor_copy(
+            w_codes[:].rearrange("p z (t m) -> p z t m", t=PACK), w_raw[:].rearrange("p z (m t) -> p z t m", t=PACK)
+        )
+        nc.vector.tensor_copy(
+            w_plane[:].rearrange("p z (t m) -> p z t m", t=PACK), ws_raw[:].rearrange("p z (m t) -> p z t m", t=PACK)
+        )
+        for h in range(HALVES):
+            round_u(nc.vector.tensor_copy, 0, h, 0, PACK)
+        for h in range(HALVES):
+            quantize_u(0, h)
+        for h in range(HALVES):
+            first_matmuls(0, h)
+
+        for e in range(2):
+            nc.tensor.transpose(bi_ps[:, e, :], bi_col[:, e : e + 1].to_broadcast([P, P]), ident[:])
+
+        for t in range(PACK):
+            pick_b(1, t)
+        nc.scalar.copy(bi_row[:].rearrange("p (m e) -> p m e", e=2), bi_ps[:].rearrange("p e m -> p m e"))
+        for t in range(PACK - 1):
+            product(1, t)
+        for h in range(HALVES):
+            round_u(nc.scalar.copy, 1, h, 0, 2)
+        for h in range(HALVES):
+            product_half(1, PACK - 1, h)
+        for h in range(HALVES):
+            round_u(nc.vector.tensor_copy, 1, h, 2, PACK)
+        for h in range(HALVES):
+            quantize_u(1, h)
+            first_matmuls(1, h)
+
+        mag0 = sb.tile([P, PACK, P], F32, name="mag0")
+        mag1 = sb.tile([P, PACK, P + 1], F32, name="mag1")
+        peak = sb.tile([P, PACK], F32, name="peak")
+        inv_peak = sb.tile([P, PACK], F32, name="inv_peak")
+        factor = sb.tile([P, PACK], F32, name="factor")
+        nc.scalar.activation(mag0[:], a_ps[0][:], ACT.Abs)
+        nc.vector.tensor_reduce(mag1[:, :, P], mag0[:], AX.X, ALU.max)
+        for i in range(2):
+            pair = slice(2 * i, 2 * i + 2)
+            nc.scalar.activation(mag1[:, pair, 0:P], a_ps[1][:, pair, :], ACT.Abs)
+            nc.vector.tensor_reduce(peak[:, pair], mag1[:, pair, :], AX.X, ALU.max)
+        nc.vector.reciprocal(inv_peak[:], peak[:])
+        nc.vector.tensor_tensor(factor[:], inv_peak[:], us_t[:], ALU.mult)
+
+        hid_bf = [sb.tile([P, P, PACK], BF16, name="hid_bf%d" % h, align_bytes=64) for h in range(HALVES)]
+        hid_codes = [sb.tile([P, P], U32, name="hid_codes%d" % h, align_bytes=64) for h in range(HALVES)]
+        hid_plane = [sb.tile([P, P], U8, name="hid_plane%d" % h, align_bytes=64) for h in range(HALVES)]
+        for h in range(HALVES):
+            nc.vector.tensor_tensor(
+                hid_bf[h][:],
+                a_ps[h][:].rearrange("p t j -> p j t"),
+                factor[:].unsqueeze(1).to_broadcast([P, P, PACK]),
+                ALU.mult,
+            )
+        for h in range(HALVES):
+            nc.vector.quantize_mx(
+                out=hid_codes[h][:].bitcast(E5M2),
+                scales=hid_plane[h][:],
+                in_=hid_bf[h][:].rearrange("p j t -> p (j t)"),
+            )
+            nc.tensor.matmul_mx(
+                out=p_ps[h][:],
+                lhsT=hid_codes[h][:].bitcast(E5M2),
+                lhsT_scale=hid_plane[h][:],
+                rhs=wb_codes[:].bitcast(E4M3),
+                rhs_scale=wb_plane[:],
+                start=True,
+                stop=True,
+            )
+
+        neg_z = [sb.tile([P, N], F32, name="neg_z%d" % h) for h in range(HALVES)]
+        low = [sb.tile([P, 1], F32, name="low%d" % h) for h in range(HALVES)]
+        ea = [sb.tile([P, N], F32, name="ea%d" % h) for h in range(HALVES)]
+        total = [sb.tile([P, 1], F32, name="total%d" % h) for h in range(HALVES)]
+        inv_total = [sb.tile([P, 1], F32, name="inv_total%d" % h) for h in range(HALVES)]
+        y = [sb.tile([P, N], F32, name="y%d" % h) for h in range(HALVES)]
+        for h in range(HALVES):
+            nc.vector.scalar_tensor_tensor(neg_z[h][:], p_ps[h][:], -0.7, bi_row[:], ALU.mult, ALU.subtract)
+        for h in range(HALVES):
+            nc.vector.tensor_reduce(low[h][:], neg_z[h][:], AX.X, ALU.min)
+            nc.scalar.activation(ea[h][:], neg_z[h][:], ACT.Exp, bias=low[h][:], scale=-1.0, accum_out=total[h][:])
+        for h in range(HALVES):
+            nc.vector.reciprocal(inv_total[h][:], total[h][:])
+            nc.vector.tensor_scalar(y[h][:], ea[h][:], inv_total[h][:], 256.0, ALU.mult, ALU.mult)
+            nc.sync.dma_start(out=out[cols(h), :], in_=y[h][:])

@@ -36,8 +36,11 @@ def tile_list_entryproducts_peakscaled_rowshares_kernel(
 
         list_a = sb.tile([P, LIST_COLS], U16, name="list_a")
         list_b = sb.tile([P, LIST_COLS], U16, name="list_b")
-        xa_t = [[sb.tile([P, T], F32, name="xa_%d_%d" % (z, t)) for t in range(PACK)] for z in range(PASSES)]
-        xb_t = [[sb.tile([P, 2, S], F32, name="xb_%d_%d" % (z, i)) for i in range(2)] for z in range(PASSES)]
+        xa_pair = [sb.tile([P, 2 * T], F32, name="xa_pair%d" % i) for i in range(2)]
+        xa_one = [sb.tile([P, T], F32, name="xa_one%d" % t) for t in range(PACK)]
+        xb_first = sb.tile([P, PACK * S], F32, name="xb_first")
+        xb_second = sb.tile([P, (PACK - 1) * S], F32, name="xb_second")
+        xb_last = sb.tile([P, S], F32, name="xb_last")
         fk_t = sb.tile([P, PASSES, PACK], F32, name="fk_t")
         us_t = sb.tile([P, PACK], F32, name="us_t")
         bi_col = sb.tile([P, 2], F32, name="bi_col")
@@ -49,56 +52,37 @@ def tile_list_entryproducts_peakscaled_rowshares_kernel(
         nc.vector.memset(ws_raw[:].bitcast(I32), 0)
         nc.vector.memset(wb_plane[:].bitcast(I32), 0)
 
-        xa_v = xa.rearrange("(z p t) c -> z t p c", p=P, t=PACK)
-        xb_v = xb.rearrange("(z p i e) c -> z i p e c", p=P, i=2, e=2)
+        xa_pairs = xa.rearrange("(z p i e) c -> z i p (e c)", p=P, i=2, e=2)
+        xa_rows = xa.rearrange("(z p t) c -> z t p c", p=P, t=PACK)
+        xb_v = xb.rearrange("(z p t) c -> z p (t c)", p=P, t=PACK)
 
-        def load_xa(z, t):
-            nc.sync.dma_start(out=xa_t[z][t][:], in_=xa_v[z, t])
-
-        def load_xb(z, i):
-            nc.sync.dma_start(out=xb_t[z][i][:], in_=xb_v[z, i])
-
-        def load_ws(q):
+        nc.sync.dma_start(out=xb_first[:], in_=xb_v[0])
+        nc.sync.dma_start(list_b[:], offs2)
+        nc.sync.dma_start(out=fk_t[:], in_=fk.rearrange("(z p t) o -> p z (t o)", p=P, t=PACK))
+        nc.sync.dma_start(out=w_raw[:].bitcast(I32), in_=w_words.rearrange("z p c -> p z c").bitcast(I32))
+        nc.sync.dma_start(out=xa_pair[0][:], in_=xa_pairs[0, 0])
+        nc.sync.dma_start(list_a[:], offs)
+        nc.sync.dma_start(out=xa_pair[1][:], in_=xa_pairs[0, 1])
+        for q in range(4):
             nc.sync.dma_start(
                 out=ws_raw[32 * q : 32 * q + 4].bitcast(I32),
                 in_=w_scales[:, 4 * q : 4 * q + 4, :].rearrange("z r c -> r z c").bitcast(I32),
             )
-
-        def load_wbs(q):
+        nc.sync.dma_start(out=xb_second[:], in_=xb_v[1][:, 0 : (PACK - 1) * S])
+        for t in range(PACK - 1):
+            nc.sync.dma_start(out=xa_one[t][:], in_=xa_rows[1, t])
+        nc.sync.dma_start(out=xb_last[:], in_=xb_v[1][:, (PACK - 1) * S : PACK * S])
+        nc.sync.dma_start(out=xa_one[PACK - 1][:], in_=xa_rows[1, PACK - 1])
+        nc.sync.dma_start(out=bi_col[:], in_=bi.rearrange("o (p e) -> p (o e)", e=2))
+        nc.sync.dma_start(out=us_t[:], in_=us.rearrange("(p t) o -> p (t o)", t=PACK))
+        nc.sync.dma_start(
+            out=wb_codes[:].bitcast(I32), in_=wb_words[0].rearrange("p n t -> p (n t)").bitcast(I32)
+        )
+        for q in range(4):
             nc.sync.dma_start(
                 out=wb_plane[32 * q : 32 * q + 4].bitcast(I32),
                 in_=wb_scales[0, 4 * q : 4 * q + 4, :].bitcast(I32),
             )
-
-        load_xb(0, 0)
-        nc.sync.dma_start(list_b[:], offs2)
-        load_xb(0, 1)
-        nc.sync.dma_start(out=fk_t[:], in_=fk.rearrange("(z p t) o -> p z (t o)", p=P, t=PACK))
-        load_xa(0, 0)
-        nc.sync.dma_start(list_a[:], offs)
-        load_xa(0, 1)
-        nc.sync.dma_start(out=w_raw[:].bitcast(I32), in_=w_words.rearrange("z p c -> p z c").bitcast(I32))
-        load_xa(0, 2)
-        load_ws(0)
-        load_ws(1)
-        load_xa(0, 3)
-        load_ws(2)
-        load_ws(3)
-        load_xb(1, 0)
-        nc.sync.dma_start(out=bi_col[:], in_=bi.rearrange("o (p e) -> p (o e)", e=2))
-        nc.sync.dma_start(out=us_t[:], in_=us.rearrange("(p t) o -> p (t o)", t=PACK))
-        load_xb(1, 1)
-        nc.sync.dma_start(
-            out=wb_codes[:].bitcast(I32), in_=wb_words[0].rearrange("p n t -> p (n t)").bitcast(I32)
-        )
-        load_xa(1, 0)
-        load_wbs(0)
-        load_wbs(1)
-        load_xa(1, 1)
-        load_wbs(2)
-        load_wbs(3)
-        load_xa(1, 2)
-        load_xa(1, 3)
 
         ident = sb.tile([P, P], F32, name="ident")
         make_identity(nc, ident[:])
@@ -110,40 +94,32 @@ def tile_list_entryproducts_peakscaled_rowshares_kernel(
             [sb.tile([P, P, PACK], BF16, name="u_bf%d_%d" % (z, h), align_bytes=64) for h in range(HALVES)]
             for z in range(PASSES)
         ]
-        u_codes = [
-            [sb.tile([P, P], U32, name="u_codes%d_%d" % (z, h), align_bytes=64) for h in range(HALVES)]
-            for z in range(PASSES)
-        ]
-        u_plane = [
-            [sb.tile([P, P], U8, name="u_plane%d_%d" % (z, h), align_bytes=64) for h in range(HALVES)]
-            for z in range(PASSES)
-        ]
+        u_codes = [sb.tile([P, J], U32, name="u_codes%d" % z, align_bytes=64) for z in range(PASSES)]
+        u_plane = [sb.tile([P, J], U8, name="u_plane%d" % z, align_bytes=64) for z in range(PASSES)]
+        picked_a = [sb.tile([P, J], F32, name="picked_a%d" % i) for i in range(2)]
         w_codes = sb.tile([P, PASSES, R], U16, name="w_codes", align_bytes=64)
         w_plane = sb.tile([P, PASSES, R], U8, name="w_plane", align_bytes=64)
-        a_ps = [ps.tile([P, PACK, P], F32, name="a_ps%d" % h) for h in range(HALVES)]
+        a_ps = [ps.tile([P, J], F32, name="a_ps%d" % t) for t in range(PACK)]
         p_ps = [ps.tile([P, N], F32, name="p_ps%d" % h) for h in range(HALVES)]
         bi_ps = ps.tile([P, 2, P], F32, name="bi_ps")
-        bi_row = sb.tile([P, N], F32, name="bi_row")
 
         def cols(h):
             return slice(h * P, (h + 1) * P)
 
-        def pick_b(z, t):
-            nc.scalar.activation(picked_b[z][:, t, :], xb_t[z][t // 2][:, t % 2, :].indirect(list_b[:]), ACT.Copy)
+        def pick_b(window, z, t):
+            nc.scalar.activation(picked_b[z][:, t, :], window.indirect(list_b[:]), ACT.Copy)
+
+        def scale_b(z, t):
             nc.scalar.activation(
                 scaled_b[z][:, t, :], picked_b[z][:, t, :], ACT.Copy, scale=fk_t[:, z, t : t + 1]
             )
 
-        def product(z, t):
-            nc.vector.tensor_tensor(prod[z][:, t, :], xa_t[z][t][:].indirect(list_a[:]), scaled_b[z][:, t, :], ALU.mult)
+        def product(window, other, z, t):
+            nc.vector.tensor_tensor(prod[z][:, t, :], window.indirect(list_a[:]), other[z][:, t, :], ALU.mult)
 
-        def product_half(z, t, h):
-            half = LIST_COLS // HALVES
-            nc.vector.tensor_tensor(
-                prod[z][:, t, cols(h)],
-                xa_t[z][t][:].indirect(list_a[:, h * half : (h + 1) * half]),
-                scaled_b[z][:, t, cols(h)],
-                ALU.mult,
+        def scale_round_u(z, h, t):
+            nc.vector.tensor_scalar(
+                u_bf[z][h][:, :, t], prod[z][:, t, cols(h)], fk_t[:, z, t : t + 1], None, ALU.mult
             )
 
         def round_u(copy, z, h, t0, t1):
@@ -151,81 +127,104 @@ def tile_list_entryproducts_peakscaled_rowshares_kernel(
 
         def quantize_u(z, h):
             nc.vector.quantize_mx(
-                out=u_codes[z][h][:].bitcast(E4M3),
-                scales=u_plane[z][h][:],
+                out=u_codes[z][:, cols(h)].bitcast(E4M3),
+                scales=u_plane[z][:, cols(h)],
                 in_=u_bf[z][h][:].rearrange("p j t -> p (j t)"),
             )
 
-        def first_matmuls(z, h):
+        def first_matmuls(z):
             for t in range(PACK):
                 nc.tensor.matmul_mx(
-                    out=a_ps[h][:, t, :],
+                    out=a_ps[t][:],
                     lhsT=w_codes[:, z, cols(t)].bitcast(E2M1),
                     lhsT_scale=w_plane[:, z, cols(t)],
-                    rhs=u_codes[z][h][:].bitcast(E4M3),
-                    rhs_scale=u_plane[z][h][:],
-                    start=(z == 0 and t == 0),
-                    stop=(z == PASSES - 1 and t == PACK - 1),
+                    rhs=u_codes[z][:].bitcast(E4M3),
+                    rhs_scale=u_plane[z][:],
+                    start=(z == 0),
+                    stop=(z == PASSES - 1),
                 )
 
-        for t in range(PACK):
-            pick_b(0, t)
-            product(0, t)
         nc.vector.tensor_copy(
             w_codes[:].rearrange("p z (t m) -> p z t m", t=PACK), w_raw[:].rearrange("p z (m t) -> p z t m", t=PACK)
         )
         nc.vector.tensor_copy(
             w_plane[:].rearrange("p z (t m) -> p z t m", t=PACK), ws_raw[:].rearrange("p z (m t) -> p z t m", t=PACK)
         )
+        for t in range(PACK):
+            pick_b(xb_first[:, t * S : (t + 1) * S], 0, t)
+            scale_b(0, t)
+        for i in range(2):
+            nc.vector.tensor_copy(picked_a[i][:], xa_pair[i][:, T : 2 * T].indirect(list_a[:]))
+            product(xa_pair[i][:], scaled_b, 0, 2 * i)
+            nc.vector.tensor_tensor(prod[0][:, 2 * i + 1, :], picked_a[i][:], scaled_b[0][:, 2 * i + 1, :], ALU.mult)
         for h in range(HALVES):
             round_u(nc.vector.tensor_copy, 0, h, 0, PACK)
         for h in range(HALVES):
             quantize_u(0, h)
-        for h in range(HALVES):
-            first_matmuls(0, h)
+        first_matmuls(0)
 
-        for e in range(2):
-            nc.tensor.transpose(bi_ps[:, e, :], bi_col[:, e : e + 1].to_broadcast([P, P]), ident[:])
-
-        for t in range(PACK):
-            pick_b(1, t)
-        nc.scalar.copy(bi_row[:].rearrange("p (m e) -> p m e", e=2), bi_ps[:].rearrange("p e m -> p m e"))
-        for t in range(PACK - 1):
-            product(1, t)
+        last = PACK - 1
+        half = LIST_COLS // HALVES
+        for t in range(2):
+            pick_b(xb_second[:, t * S : (t + 1) * S], 1, t)
+            scale_b(1, t)
+            product(xa_one[t][:], scaled_b, 1, t)
+        pick_b(xb_second[:, 2 * S : 3 * S], 1, 2)
         for h in range(HALVES):
             round_u(nc.scalar.copy, 1, h, 0, 2)
+        product(xa_one[2][:], picked_b, 1, 2)
         for h in range(HALVES):
-            product_half(1, PACK - 1, h)
-        for h in range(HALVES):
-            round_u(nc.vector.tensor_copy, 1, h, 2, PACK)
-        for h in range(HALVES):
-            quantize_u(1, h)
-            first_matmuls(1, h)
-
-        mag0 = sb.tile([P, PACK, P], F32, name="mag0")
-        mag1 = sb.tile([P, PACK, P + 1], F32, name="mag1")
-        peak = sb.tile([P, PACK], F32, name="peak")
-        inv_peak = sb.tile([P, PACK], F32, name="inv_peak")
-        factor = sb.tile([P, PACK], F32, name="factor")
-        nc.scalar.activation(mag0[:], a_ps[0][:], ACT.Abs)
-        nc.vector.tensor_reduce(mag1[:, :, P], mag0[:], AX.X, ALU.max)
-        for i in range(2):
-            pair = slice(2 * i, 2 * i + 2)
-            nc.scalar.activation(mag1[:, pair, 0:P], a_ps[1][:, pair, :], ACT.Abs)
-            nc.vector.tensor_reduce(peak[:, pair], mag1[:, pair, :], AX.X, ALU.max)
-        nc.vector.reciprocal(inv_peak[:], peak[:])
-        nc.vector.tensor_tensor(factor[:], inv_peak[:], us_t[:], ALU.mult)
-
-        hid_bf = [sb.tile([P, P, PACK], BF16, name="hid_bf%d" % h, align_bytes=64) for h in range(HALVES)]
-        hid_codes = [sb.tile([P, P], U32, name="hid_codes%d" % h, align_bytes=64) for h in range(HALVES)]
-        hid_plane = [sb.tile([P, P], U8, name="hid_plane%d" % h, align_bytes=64) for h in range(HALVES)]
+            scale_round_u(1, h, 2)
+        pick_b(xb_last[:], 1, last)
         for h in range(HALVES):
             nc.vector.tensor_tensor(
-                hid_bf[h][:],
-                a_ps[h][:].rearrange("p t j -> p j t"),
-                factor[:].unsqueeze(1).to_broadcast([P, P, PACK]),
+                prod[1][:, last, cols(h)],
+                xa_one[last][:].indirect(list_a[:, h * half : (h + 1) * half]),
+                picked_b[1][:, last, cols(h)],
                 ALU.mult,
             )
+        for h in range(HALVES):
+            scale_round_u(1, h, last)
+        for h in range(HALVES):
+            quantize_u(1, h)
+        for e in range(2):
+            nc.tensor.transpose(bi_ps[:, e, :], bi_col[:, e : e + 1].to_broadcast([P, P]), ident[:])
+        bi_row = sb.tile([P, N], F32, name="bi_row")
+        nc.scalar.copy(bi_row[:].rearrange("p (m e) -> p m e", e=2), bi_ps[:].rearrange("p e m -> p m e"))
+        for t in range(PACK):
+            for h in range(HALVES):
+                nc.tensor.matmul_mx(
+                    out=a_ps[t][:, cols(h)],
+                    lhsT=w_codes[:, 1, cols(t)].bitcast(E2M1),
+                    lhsT_scale=w_plane[:, 1, cols(t)],
+                    rhs=u_codes[1][:, cols(h)].bitcast(E4M3),
+                    rhs_scale=u_plane[1][:, cols(h)],
+                    start=False,
+                    stop=(h == HALVES - 1),
+                )
+
+        a_sb = [sb.tile([P, J], F32, name="a_sb%d" % t) for t in range(PACK)]
+        peak = [sb.tile([P, 1], F32, name="peak%d" % t) for t in range(PACK)]
+        inv_peak = [sb.tile([P, 1], F32, name="inv_peak%d" % t) for t in range(PACK)]
+        factor = [sb.tile([P, 1], F32, name="factor%d" % t) for t in range(2)]
+        hid_bf = [sb.tile([P, P, PACK], BF16, name="hid_bf%d" % h, align_bytes=64) for h in range(HALVES)]
+        for t in range(PACK):
+            nc.scalar.copy(a_sb[t][:], a_ps[t][:])
+        for t in range(PACK):
+            nc.vector.tensor_reduce(peak[t][:], a_sb[t][:], AX.X, ALU.max, apply_absolute_value=True)
+            nc.vector.reciprocal(inv_peak[t][:], peak[t][:])
+            if t < 2:
+                nc.vector.tensor_tensor(factor[t][:], inv_peak[t][:], us_t[:, t : t + 1], ALU.mult)
+                for h in range(HALVES):
+                    nc.scalar.activation(hid_bf[h][:, :, t], a_sb[t][:, cols(h)], ACT.Copy, scale=factor[t][:])
+        for t in range(2, PACK):
+            for h in range(HALVES):
+                nc.vector.tensor_scalar(
+                    hid_bf[h][:, :, t], a_sb[t][:, cols(h)], inv_peak[t][:], us_t[:, t : t + 1], ALU.mult, ALU.mult
+                )
+
+        hid_codes = [sb.tile([P, P], U32, name="hid_codes%d" % h, align_bytes=64) for h in range(HALVES)]
+        hid_plane = [sb.tile([P, P], U8, name="hid_plane%d" % h, align_bytes=64) for h in range(HALVES)]
         for h in range(HALVES):
             nc.vector.quantize_mx(
                 out=hid_codes[h][:].bitcast(E5M2),

@@ -49,7 +49,12 @@ def tile_list_entryproducts_peakscaled_rowshares_kernel(
         wb_codes = sb.tile([P, N], U32, name="wb_codes", align_bytes=64)
         wb_plane = sb.tile([P, N], U8, name="wb_plane", align_bytes=64)
 
-        nc.vector.memset(ws_raw[:].bitcast(I32), 0)
+        nc.gpsimd.memset(ws_raw[:].bitcast(I32), 0)
+        for q in range(4):
+            nc.gpsimd.dma_start(
+                out=ws_raw[32 * q : 32 * q + 4].bitcast(I32),
+                in_=w_scales[:, 4 * q : 4 * q + 4, :].rearrange("z r c -> r z c").bitcast(I32),
+            )
         nc.vector.memset(wb_plane[:].bitcast(I32), 0)
 
         xa_pairs = xa.rearrange("(z p i e) c -> z i p (e c)", p=P, i=2, e=2)
@@ -63,11 +68,6 @@ def tile_list_entryproducts_peakscaled_rowshares_kernel(
         nc.sync.dma_start(out=xa_pair[0][:], in_=xa_pairs[0, 0])
         nc.sync.dma_start(list_a[:], offs)
         nc.sync.dma_start(out=xa_pair[1][:], in_=xa_pairs[0, 1])
-        for q in range(4):
-            nc.sync.dma_start(
-                out=ws_raw[32 * q : 32 * q + 4].bitcast(I32),
-                in_=w_scales[:, 4 * q : 4 * q + 4, :].rearrange("z r c -> r z c").bitcast(I32),
-            )
         nc.sync.dma_start(out=xb_second[:], in_=xb_v[1][:, 0 : (PACK - 1) * S])
         for t in range(PACK - 1):
             nc.sync.dma_start(out=xa_one[t][:], in_=xa_rows[1, t])

@@ -50,11 +50,6 @@ def tile_list_entryproducts_peakscaled_rowshares_kernel(
         wb_plane = sb.tile([P, N], U8, name="wb_plane", align_bytes=64)
 
         nc.gpsimd.memset(ws_raw[:].bitcast(I32), 0)
-        for q in range(4):
-            nc.gpsimd.dma_start(
-                out=ws_raw[32 * q : 32 * q + 4].bitcast(I32),
-                in_=w_scales[:, 4 * q : 4 * q + 4, :].rearrange("z r c -> r z c").bitcast(I32),
-            )
         nc.vector.memset(wb_plane[:].bitcast(I32), 0)
 
         xa_pairs = xa.rearrange("(z p i e) c -> z i p (e c)", p=P, i=2, e=2)
@@ -64,9 +59,14 @@ def tile_list_entryproducts_peakscaled_rowshares_kernel(
         nc.sync.dma_start(out=xb_first[:], in_=xb_v[0])
         nc.sync.dma_start(list_b[:], offs2)
         nc.sync.dma_start(out=fk_t[:], in_=fk.rearrange("(z p t) o -> p z (t o)", p=P, t=PACK))
-        nc.sync.dma_start(out=w_raw[:].bitcast(I32), in_=w_words.rearrange("z p c -> p z c").bitcast(I32))
+        for q in range(4):
+            nc.sync.dma_start(
+                out=ws_raw[32 * q : 32 * q + 4].bitcast(I32),
+                in_=w_scales[:, 4 * q : 4 * q + 4, :].rearrange("z r c -> r z c").bitcast(I32),
+            )
         nc.sync.dma_start(out=xa_pair[0][:], in_=xa_pairs[0, 0])
         nc.sync.dma_start(list_a[:], offs)
+        nc.sync.dma_start(out=w_raw[:].bitcast(I32), in_=w_words.rearrange("z p c -> p z c").bitcast(I32))
         nc.sync.dma_start(out=xa_pair[1][:], in_=xa_pairs[0, 1])
         nc.sync.dma_start(out=xb_second[:], in_=xb_v[1][:, 0 : (PACK - 1) * S])
         for t in range(PACK - 1):
@@ -145,18 +145,22 @@ def tile_list_entryproducts_peakscaled_rowshares_kernel(
                 )
 
         nc.vector.tensor_copy(
-            w_codes[:].rearrange("p z (t m) -> p z t m", t=PACK), w_raw[:].rearrange("p z (m t) -> p z t m", t=PACK)
-        )
-        nc.vector.tensor_copy(
             w_plane[:].rearrange("p z (t m) -> p z t m", t=PACK), ws_raw[:].rearrange("p z (m t) -> p z t m", t=PACK)
         )
         for t in range(PACK):
             pick_b(xb_first[:, t * S : (t + 1) * S], 0, t)
             scale_b(0, t)
         for i in range(2):
-            nc.vector.tensor_copy(picked_a[i][:], xa_pair[i][:, T : 2 * T].indirect(list_a[:]))
+            second_row = xa_pair[i][:, T : 2 * T].indirect(list_a[:])
+            if i == 0:
+                nc.vector.tensor_copy(picked_a[i][:], second_row)
+            else:
+                nc.scalar.activation(picked_a[i][:], second_row, ACT.Copy)
             product(xa_pair[i][:], scaled_b, 0, 2 * i)
             nc.vector.tensor_tensor(prod[0][:, 2 * i + 1, :], picked_a[i][:], scaled_b[0][:, 2 * i + 1, :], ALU.mult)
+        nc.vector.tensor_copy(
+            w_codes[:].rearrange("p z (t m) -> p z t m", t=PACK), w_raw[:].rearrange("p z (m t) -> p z t m", t=PACK)
+        )
         for h in range(HALVES):
             round_u(nc.vector.tensor_copy, 0, h, 0, PACK)
         for h in range(HALVES):

from contextlib import ExitStack

import concourse.mybir as mybir
from concourse.masks import make_identity

K, T, J, S, R, N = 1024, 1024, 256, 512, 512, 256
FLOPS = 2 * K * R * J + 2 * R * J * N

F32 = mybir.dt.float32
BF16 = mybir.dt.bfloat16
I32 = mybir.dt.int32
U32 = mybir.dt.uint32
U16 = mybir.dt.uint16
U8 = mybir.dt.uint8
E4M3 = mybir.dt.float8_e4m3fn_x4
E5M2 = mybir.dt.float8_e5m2_x4
E2M1 = mybir.dt.float4_e2m1fn_x4
ALU = mybir.AluOpType
ACT = mybir.ActivationFunctionType
AX = mybir.AxisListType

P = 128
PACK = 4
PASSES = K // (P * PACK)
HALVES = J // P
LIST_COLS = J // 16


def tile_list_entryproducts_peakscaled_rowshares_kernel(
    tc, xa, xb, fk, w_words, w_scales, us, wb_words, wb_scales, bi, offs, offs2, out
):
    nc = tc.nc
    with ExitStack() as ctx:
        sb = ctx.enter_context(tc.tile_pool(name="sb", bufs=1))
        ps = ctx.enter_context(tc.psum_pool(name="ps", bufs=1))

        list_a = sb.tile([P, LIST_COLS], U16, name="list_a")
        list_b = sb.tile([P, LIST_COLS], U16, name="list_b")
        xa_pair = [sb.tile([P, 2 * T], F32, name="xa_pair%d" % i) for i in range(2)]
        xa_one = [sb.tile([P, T], F32, name="xa_one%d" % t) for t in range(PACK)]
        xb_first = sb.tile([P, PACK * S], F32, name="xb_first")
        xb_second = sb.tile([P, (PACK - 1) * S], F32, name="xb_second")
        xb_last = sb.tile([P, S], F32, name="xb_last")
        fk_t = sb.tile([P, PASSES, PACK], F32, name="fk_t")
        us_t = sb.tile([P, PACK], F32, name="us_t")
        bi_col = sb.tile([P, 2], F32, name="bi_col")
        w_raw = sb.tile([P, PASSES, R], U16, name="w_raw", align_bytes=64)
        ws_raw = sb.tile([P, PASSES, R], U8, name="ws_raw", align_bytes=64)
        wb_codes = sb.tile([P, N], U32, name="wb_codes", align_bytes=64)
        wb_plane = sb.tile([P, N], U8, name="wb_plane", align_bytes=64)

        nc.gpsimd.memset(ws_raw[:].bitcast(I32), 0)
        nc.vector.memset(wb_plane[:].bitcast(I32), 0)

        xa_pairs = xa.rearrange("(z p i e) c -> z i p (e c)", p=P, i=2, e=2)
        xa_rows = xa.rearrange("(z p t) c -> z t p c", p=P, t=PACK)
        xb_v = xb.rearrange("(z p t) c -> z p (t c)", p=P, t=PACK)

        nc.sync.dma_start(out=xb_first[:], in_=xb_v[0])
        nc.sync.dma_start(list_b[:], offs2)
        nc.sync.dma_start(out=fk_t[:], in_=fk.rearrange("(z p t) o -> p z (t o)", p=P, t=PACK))
        for q in range(4):
            nc.sync.dma_start(
                out=ws_raw[32 * q : 32 * q + 4].bitcast(I32),
                in_=w_scales[:, 4 * q : 4 * q + 4, :].rearrange("z r c -> r z c").bitcast(I32),
            )
        nc.sync.dma_start(out=xa_pair[0][:], in_=xa_pairs[0, 0])
        nc.sync.dma_start(list_a[:], offs)
        nc.sync.dma_start(out=w_raw[:].bitcast(I32), in_=w_words.rearrange("z p c -> p z c").bitcast(I32))
        nc.sync.dma_start(out=xa_pair[1][:], in_=xa_pairs[0, 1])
        nc.sync.dma_start(out=xb_second[:], in_=xb_v[1][:, 0 : (PACK - 1) * S])
        for t in range(PACK - 1):
            nc.sync.dma_start(out=xa_one[t][:], in_=xa_rows[1, t])
        nc.sync.dma_start(out=xb_last[:], in_=xb_v[1][:, (PACK - 1) * S : PACK * S])
        nc.sync.dma_start(out=xa_one[PACK - 1][:], in_=xa_rows[1, PACK - 1])
        nc.sync.dma_start(out=bi_col[:], in_=bi.rearrange("o (p e) -> p (o e)", e=2))
        nc.sync.dma_start(out=us_t[:], in_=us.rearrange("(p t) o -> p (t o)", t=PACK))
        nc.sync.dma_start(
            out=wb_codes[:].bitcast(I32), in_=wb_words[0].rearrange("p n t -> p (n t)").bitcast(I32)
        )
        for q in range(4):
            nc.sync.dma_start(
                out=wb_plane[32 * q : 32 * q + 4].bitcast(I32),
                in_=wb_scales[0, 4 * q : 4 * q + 4, :].bitcast(I32),
            )

        ident = sb.tile([P, P], F32, name="ident")
        make_identity(nc, ident[:])

        picked_b = [sb.tile([P, PACK, J], F32, name="picked_b%d" % z) for z in range(PASSES)]
        scaled_b = [sb.tile([P, PACK, J], F32, name="scaled_b%d" % z) for z in range(PASSES)]
        prod = [sb.tile([P, PACK, J], F32, name="prod%d" % z) for z in range(PASSES)]
        u_bf = [
            [sb.tile([P, P, PACK], BF16, name="u_bf%d_%d" % (z, h), align_bytes=64) for h in range(HALVES)]
            for z in range(PASSES)
        ]
        u_codes = [sb.tile([P, J], U32, name="u_codes%d" % z, align_bytes=64) for z in range(PASSES)]
        u_plane = [sb.tile([P, J], U8, name="u_plane%d" % z, align_bytes=64) for z in range(PASSES)]
        picked_a = [sb.tile([P, J], F32, name="picked_a%d" % i) for i in range(2)]
        w_codes = sb.tile([P, PASSES, R], U16, name="w_codes", align_bytes=64)
        w_plane = sb.tile([P, PASSES, R], U8, name="w_plane", align_bytes=64)
        a_ps = [ps.tile([P, J], F32, name="a_ps%d" % t) for t in range(PACK)]
        p_ps = [ps.tile([P, N], F32, name="p_ps%d" % h) for h in range(HALVES)]
        bi_ps = ps.tile([P, 2, P], F32, name="bi_ps")

        def cols(h):
            return slice(h * P, (h + 1) * P)

        def pick_b(window, z, t):
            nc.scalar.activation(picked_b[z][:, t, :], window.indirect(list_b[:]), ACT.Copy)

        def scale_b(z, t):
            nc.scalar.activation(
                scaled_b[z][:, t, :], picked_b[z][:, t, :], ACT.Copy, scale=fk_t[:, z, t : t + 1]
            )

        def product(window, other, z, t):
            nc.vector.tensor_tensor(prod[z][:, t, :], window.indirect(list_a[:]), other[z][:, t, :], ALU.mult)

        def scale_round_u(z, h, t):
            nc.vector.tensor_scalar(
                u_bf[z][h][:, :, t], prod[z][:, t, cols(h)], fk_t[:, z, t : t + 1], None, ALU.mult
            )

        def round_u(copy, z, h, t0, t1):
            copy(u_bf[z][h][:, :, t0:t1], prod[z][:, t0:t1, cols(h)].rearrange("p t j -> p j t"))

        def quantize_u(z, h):
            nc.vector.quantize_mx(
                out=u_codes[z][:, cols(h)].bitcast(E4M3),
                scales=u_plane[z][:, cols(h)],
                in_=u_bf[z][h][:].rearrange("p j t -> p (j t)"),
            )

        def first_matmuls(z):
            for t in range(PACK):
                nc.tensor.matmul_mx(
                    out=a_ps[t][:],
                    lhsT=w_codes[:, z, cols(t)].bitcast(E2M1),
                    lhsT_scale=w_plane[:, z, cols(t)],
                    rhs=u_codes[z][:].bitcast(E4M3),
                    rhs_scale=u_plane[z][:],
                    start=(z == 0),
                    stop=(z == PASSES - 1),
                )

        nc.vector.tensor_copy(
            w_plane[:].rearrange("p z (t m) -> p z t m", t=PACK), ws_raw[:].rearrange("p z (m t) -> p z t m", t=PACK)
        )
        for t in range(PACK):
            pick_b(xb_first[:, t * S : (t + 1) * S], 0, t)
            scale_b(0, t)
        for i in range(2):
            second_row = xa_pair[i][:, T : 2 * T].indirect(list_a[:])
            if i == 0:
                nc.vector.tensor_copy(picked_a[i][:], second_row)
            else:
                nc.scalar.activation(picked_a[i][:], second_row, ACT.Copy)
            product(xa_pair[i][:], scaled_b, 0, 2 * i)
            nc.vector.tensor_tensor(prod[0][:, 2 * i + 1, :], picked_a[i][:], scaled_b[0][:, 2 * i + 1, :], ALU.mult)
        nc.vector.tensor_copy(
            w_codes[:].rearrange("p z (t m) -> p z t m", t=PACK), w_raw[:].rearrange("p z (m t) -> p z t m", t=PACK)
        )
        for h in range(HALVES):
            round_u(nc.vector.tensor_copy, 0, h, 0, PACK)
        for h in range(HALVES):
            quantize_u(0, h)
        first_matmuls(0)

        last = PACK - 1
        half = LIST_COLS // HALVES
        for t in range(2):
            pick_b(xb_second[:, t * S : (t + 1) * S], 1, t)
            scale_b(1, t)
            product(xa_one[t][:], scaled_b, 1, t)
        pick_b(xb_second[:, 2 * S : 3 * S], 1, 2)
        for h in range(HALVES):
            round_u(nc.scalar.copy, 1, h, 0, 2)
        product(xa_one[2][:], picked_b, 1, 2)
        for h in range(HALVES):
            scale_round_u(1, h, 2)
        pick_b(xb_last[:], 1, last)
        for h in range(HALVES):
            nc.vector.tensor_tensor(
                prod[1][:, last, cols(h)],
                xa_one[last][:].indirect(list_a[:, h * half : (h + 1) * half]),
                picked_b[1][:, last, cols(h)],
                ALU.mult,
            )
        for h in range(HALVES):
            scale_round_u(1, h, last)
        for h in range(HALVES):
            quantize_u(1, h)
        for e in range(2):
            nc.tensor.transpose(bi_ps[:, e, :], bi_col[:, e : e + 1].to_broadcast([P, P]), ident[:])
        bi_row = sb.tile([P, N], F32, name="bi_row")
        nc.scalar.copy(bi_row[:].rearrange("p (m e) -> p m e", e=2), bi_ps[:].rearrange("p e m -> p m e"))
        for t in range(PACK):
            for h in range(HALVES):
                nc.tensor.matmul_mx(
                    out=a_ps[t][:, cols(h)],
                    lhsT=w_codes[:, 1, cols(t)].bitcast(E2M1),
                    lhsT_scale=w_plane[:, 1, cols(t)],
                    rhs=u_codes[1][:, cols(h)].bitcast(E4M3),
                    rhs_scale=u_plane[1][:, cols(h)],
                    start=False,
                    stop=(h == HALVES - 1),
                )

        a_sb = [sb.tile([P, J], F32, name="a_sb%d" % t) for t in range(PACK)]
        peak = [sb.tile([P, 1], F32, name="peak%d" % t) for t in range(PACK)]
        inv_peak = [sb.tile([P, 1], F32, name="inv_peak%d" % t) for t in range(PACK)]
        factor = [sb.tile([P, 1], F32, name="factor%d" % t) for t in range(2)]
        hid_bf = [sb.tile([P, P, PACK], BF16, name="hid_bf%d" % h, align_bytes=64) for h in range(HALVES)]
        for t in range(PACK):
            nc.scalar.copy(a_sb[t][:], a_ps[t][:])
        for t in range(PACK):
            nc.vector.tensor_reduce(peak[t][:], a_sb[t][:], AX.X, ALU.max, apply_absolute_value=True)
            nc.vector.reciprocal(inv_peak[t][:], peak[t][:])
            if t < 2:
                nc.vector.tensor_tensor(factor[t][:], inv_peak[t][:], us_t[:, t : t + 1], ALU.mult)
                for h in range(HALVES):
                    nc.scalar.activation(hid_bf[h][:, :, t], a_sb[t][:, cols(h)], ACT.Copy, scale=factor[t][:])
        for t in range(2, PACK):
            for h in range(HALVES):
                nc.vector.tensor_scalar(
                    hid_bf[h][:, :, t], a_sb[t][:, cols(h)], inv_peak[t][:], us_t[:, t : t + 1], ALU.mult, ALU.mult
                )

        hid_codes = [sb.tile([P, P], U32, name="hid_codes%d" % h, align_bytes=64) for h in range(HALVES)]
        hid_plane = [sb.tile([P, P], U8, name="hid_plane%d" % h, align_bytes=64) for h in range(HALVES)]
        for h in range(HALVES):
            nc.vector.quantize_mx(
                out=hid_codes[h][:].bitcast(E5M2),
                scales=hid_plane[h][:],
                in_=hid_bf[h][:].rearrange("p j t -> p (j t)"),
            )
            nc.tensor.matmul_mx(
                out=p_ps[h][:],
                lhsT=hid_codes[h][:].bitcast(E5M2),
                lhsT_scale=hid_plane[h][:],
                rhs=wb_codes[:].bitcast(E4M3),
                rhs_scale=wb_plane[:],
                start=True,
                stop=True,
            )

        neg_z = [sb.tile([P, N], F32, name="neg_z%d" % h) for h in range(HALVES)]
        low = [sb.tile([P, 1], F32, name="low%d" % h) for h in range(HALVES)]
        ea = [sb.tile([P, N], F32, name="ea%d" % h) for h in range(HALVES)]
        total = [sb.tile([P, 1], F32, name="total%d" % h) for h in range(HALVES)]
        inv_total = [sb.tile([P, 1], F32, name="inv_total%d" % h) for h in range(HALVES)]
        y = [sb.tile([P, N], F32, name="y%d" % h) for h in range(HALVES)]
        for h in range(HALVES):
            nc.vector.scalar_tensor_tensor(neg_z[h][:], p_ps[h][:], -0.7, bi_row[:], ALU.mult, ALU.subtract)
        for h in range(HALVES):
            nc.vector.tensor_reduce(low[h][:], neg_z[h][:], AX.X, ALU.min)
            nc.scalar.activation(ea[h][:], neg_z[h][:], ACT.Exp, bias=low[h][:], scale=-1.0, accum_out=total[h][:])
        for h in range(HALVES):
            nc.vector.reciprocal(inv_total[h][:], total[h][:])
            nc.vector.tensor_scalar(y[h][:], ea[h][:], inv_total[h][:], 256.0, ALU.mult, ALU.mult)
            nc.sync.dma_start(out=out[cols(h), :], in_=y[h][:])
